import numpy as np, ml_dtypes
CORES = [36,164,52,180,100,228,116,244]
N = 8
import mx_ref
NC, GR, GC, KT = 128, 4, 2, 2
TS = GC * KT
CH = GR * NC // GC
BF = ml_dtypes.bfloat16
def setup_inputs(rng):
    def f(*shape):
        return mx_ref.flush((rng.standard_normal(shape, dtype=np.float32) * np.exp2(rng.integers(-2, 3, shape[:-1] + (1,)))).astype(BF))
    return {"w": f(N, 128, KT * 512), "x": f(N, 128, KT * 4 * NC)}
def setup_inputs_blocks(rng):
    d = setup_inputs(rng)
    for k in ("w", "x"): d[k] = mx_ref.spread(d[k], rng, 1)
    return d
def setup_inputs_wide(rng):
    d = setup_inputs(rng)
    for k in ("w", "x"): d[k] = mx_ref.flush((d[k].astype(np.float32) * np.exp2(rng.integers(-8, 9, (N, 1, 1))).astype(np.float32)).astype(BF))
    return d
def setup_inputs_zeros(rng):
    d = setup_inputs(rng); v = d["x"].reshape(N, 128, -1, 4).copy()
    v[np.broadcast_to((rng.random((N, 1, v.shape[2], 1)) < 0.33), v.shape)] = 0
    d["x"] = v.reshape(d["x"].shape)
    return d
def reference(w, x):
    QX = [[mx_ref.quantize(x[r][:, 4 * NC * t:4 * NC * t + 4 * NC]) for t in range(KT)] for r in range(N)]
    y = np.zeros((N, 128, CH), np.float32)
    for i in range(GR):
        for s in range(TS):
            k, t = s // KT, s % KT
            qw = mx_ref.quantize(w[i * GC + k][:, 512 * t:512 * t + 512])
            p = np.concatenate([mx_ref.matmul(qw, QX[g * GC + k][t]) for g in range(GR)], axis=1)
            Y = p if s == 0 else Y + p
        for c in range(GC):
            y[i * GC + c] = Y[:, CH * c:CH * c + CH]
    return {"y": y}

@@ -1,0 +1,168 @@
+from concourse.bass import DstId, RemoteDMATransfer
+from concourse.mybir import dt, ActivationFunctionType
+
+GR, GC, KT, NC = 4, 2, 2, 128
+N = GR * GC
+U = KT * NC
+GH = GR // GC
+SLOTS = GH * GC + GC - 1
+
+SCRATCH = {
+    "xin": ("sbuf", [128, 4 * U], "bfloat16"),
+    "win": ("sbuf", [128, 4 * U], "bfloat16"),
+    "q": ("sbuf", [128, 2 * U], "float8_e4m3fn_x4"),
+    "s": ("sbuf", [128, 2 * U], "uint8"),
+    "rq": ("sbuf", [128, SLOTS * U], "float8_e4m3fn_x4"),
+    "rs": ("sbuf", [128, SLOTS * U], "uint8"),
+    "acc": ("psum", [128, 512 * GH], "float32"),
+    "out": ("sbuf", [128, GH * NC], "float32"),
+}
+SEMAPHORES = ["ldx", "ldw", "qx", "qw", "sent", "mm0", "mm1", "ev0", "ev1", "st0", "st1"] + ["a%d" % r for r in range(N)]
+
+
+def _rank(i, k):
+    return i * GC + k
+
+
+def _x_sources(r):
+    c = r % GC
+    return [_rank(g, k) for g in range(c * GH, (c + 1) * GH) for k in range(GC)]
+
+
+def _w_sources(r):
+    return [_rank(r // GC, k) for k in range(GC)]
+
+
+def _landing(r):
+    xs = [s for s in _x_sources(r) if s != r]
+    ws = [s for s in _w_sources(r) if s != r]
+    order = [("x", s) for s in xs if s not in ws]
+    for s in ws:
+        if s in xs:
+            order.append(("x", s))
+        order.append(("w", s))
+    return {key: U * j for j, key in enumerate(order)}
+
+
+def _calls(s):
+    xd = [d for d in range(N) if d != s and s in _x_sources(d)]
+    wd = [d for d in range(N) if d != s and s in _w_sources(d)]
+
+    def x_to(ds):
+        return (0, U, [(d, _landing(d)[("x", s)]) for d in ds])
+    if [d for d in wd if d in xd]:
+        calls = [x_to([d for d in xd if d not in wd and d not in _x_sources(d)])]
+        calls += [(0, 2 * U, [(d, _landing(d)[("x", s)])]) for d in wd]
+        calls += [x_to([d for d in xd if d not in wd and d in _x_sources(d)])]
+    else:
+        calls = [(U, 2 * U, [(d, _landing(d)[("w", s)])]) for d in wd] + [x_to(xd)]
+    out, sent = [], 0
+    for a, b, dests in calls:
+        sent += (b - a) // U * len(dests)
+        out.append((a, b, dests, sent))
+    return out
+
+
+def _mask(topo, cores, s, dests):
+    m = topo.mask(cores[s], cores[dests[0][0]])
+    for d, _ in dests:
+        m &= topo.mask(cores[s], cores[d])
+    return m
+
+
+def _ones(m):
+    return bin(m).count("1")
+
+
+def rank_program(g, core, T, topo):
+    r = T.rank_of(core)
+    if r is None:
+        return
+    i, c = r // GC, r % GC
+    sem = T.sem
+    calls = _calls(r)
+
+    inputs = [("x", T.x, T.xin, 0), ("w", T.w, T.win, U)]
+    if calls[0][0] >= U:
+        inputs.reverse()
+    for name, src, tile, off in inputs:
+        g.sync.dma_start(tile[:], src[:]).then_inc(sem["ld" + name], 16)
+    for name, src, tile, off in inputs:
+        g.vector.wait_ge(sem["ld" + name], 16)
+        for t in range(KT):
+            o = off + NC * t
+            g.vector.quantize_mx(T.q[:, o:o + NC], T.s[:, o:o + NC], tile[:, 4 * NC * t:4 * NC * (t + 1)]).then_inc(sem["q" + name], 1)
+
+    left = 0
+    ready = set()
+    for a, b, dests, _ in calls:
+        for name, need in (("qx", a < U), ("qw", b > U)):
+            if need and name not in ready:
+                ready.add(name)
+                g.wait_ge(sem[name], KT)
+        m = _mask(topo, T.cores, r, dests)
+        ids = []
+        for d, _ in dests:
+            rid, pid = topo.addr(T.cores[d], core)
+            ids.append(DstId(rid=rid, pnc=pid))
+        g.remote_dma_fused([RemoteDMATransfer(
+            dst_ids=ids, dma_engine_mask=m, remote_sem=sem["a%d" % r],
+            srcs=[T.s[:, a:b]], dsts=[T.rs[:, o:o + b - a] for _, o in dests])], local_sem=sem.sent)
+        g.remote_dma_fused([RemoteDMATransfer(
+            dst_ids=ids, dma_engine_mask=m, remote_sem=sem["a%d" % r],
+            srcs=[T.q[:, a:b].bitcast(dt.uint8)], dsts=[T.rq[:, o:o + b - a].bitcast(dt.uint8) for _, o in dests])], local_sem=sem.sent)
+        left += 2 * _ones(m)
+
+    land = _landing(r)
+    arrive = {}
+    for s in range(N):
+        for a, b, dests, sent in _calls(s):
+            if s != r and r in [d for d, _ in dests]:
+                arrive[s] = (2 * _ones(_mask(topo, T.cores, s, dests)), sent)
+    prods = []
+    for gi in range(GH):
+        for k in range(GC):
+            xs, ws = _rank(c * GH + gi, k), _rank(i, k)
+            prods.append((max([arrive[s][1] for s in (xs, ws) if s != r] + [0]), gi, xs, ws))
+    prods.sort()
+    done = set()
+    count = [0] * GH
+    finish = []
+    for _, gi, xs, ws in prods:
+        for name, s in (("qx", xs), ("qw", ws)):
+            key = name if s == r else s
+            if key not in done:
+                done.add(key)
+                if s == r:
+                    g.tensor.wait_ge(sem[name], KT)
+                else:
+                    g.tensor.wait_ge(sem["a%d" % s], arrive[s][0])
+        for t in range(KT):
+            if ws == r:
+                wq, wsc, wo = T.q, T.s, U + NC * t
+            else:
+                wq, wsc, wo = T.rq, T.rs, land[("w", ws)] + NC * t
+            if xs == r:
+                xq, xsc, xo = T.q, T.s, NC * t
+            else:
+                xq, xsc, xo = T.rq, T.rs, land[("x", xs)] + NC * t
+            count[gi] += 1
+            mm = g.tensor.matmul_mx(T.acc[:, 512 * gi:512 * gi + NC], wq[:, wo:wo + NC], wsc[:, wo:wo + NC],
+                                    xq[:, xo:xo + NC], xsc[:, xo:xo + NC], count[gi] == 1, count[gi] == GC * KT)
+            if count[gi] == GC * KT:
+                mm.then_inc(sem["mm%d" % len(finish)], 1)
+                finish.append(gi)
+
+    gi = finish[0]
+    g.vector.wait_ge(sem.mm0, 1)
+    g.vector.tensor_copy(T.out[:, NC * gi:NC * gi + NC], T.acc[:, 512 * gi:512 * gi + NC]).then_inc(sem.ev0, 1)
+    g.sync.wait_ge(sem.ev0, 1)
+    g.sync.dma_start(T.y[:, NC * gi:NC * gi + NC], T.out[:, NC * gi:NC * gi + NC]).then_inc(sem.st0, 16)
+    gi = finish[1]
+    g.scalar.wait_ge(sem.mm1, 1)
+    g.scalar.activation(T.out[:, NC * gi:NC * gi + NC], T.acc[:, 512 * gi:512 * gi + NC], ActivationFunctionType.Copy).then_inc(sem.ev1, 1)
+    g.scalar.wait_ge(sem.ev1, 1)
+    g.scalar.dma_start(T.y[:, NC * gi:NC * gi + NC], T.out[:, NC * gi:NC * gi + NC]).then_inc(sem.st1, 16)
+    g.sync.wait_ge(sem.st0, 16)
+    g.scalar.wait_ge(sem.st1, 16)
+    g.wait_ge(sem.sent, left)

@@ -1,168 +1,156 @@
 from concourse.bass import DstId, RemoteDMATransfer
-from concourse.mybir import dt, ActivationFunctionType
+from concourse.mybir import dt, ActivationFunctionType, AluOpType
 
 GR, GC, KT, NC = 4, 2, 2, 128
 N = GR * GC
+WORLD = 256
 U = KT * NC
 GH = GR // GC
-SLOTS = GH * GC + GC - 1
 
 SCRATCH = {
     "xin": ("sbuf", [128, 4 * U], "bfloat16"),
     "win": ("sbuf", [128, 4 * U], "bfloat16"),
     "q": ("sbuf", [128, 2 * U], "float8_e4m3fn_x4"),
     "s": ("sbuf", [128, 2 * U], "uint8"),
-    "rq": ("sbuf", [128, SLOTS * U], "float8_e4m3fn_x4"),
-    "rs": ("sbuf", [128, SLOTS * U], "uint8"),
-    "acc": ("psum", [128, 512 * GH], "float32"),
+    "rq": ("sbuf", [128, (GR - 1) * U], "float8_e4m3fn_x4"),
+    "rs": ("sbuf", [128, (GR - 1) * U], "uint8"),
+    "acc": ("psum", [128, 512 * GR], "float32"),
+    "fo": ("sbuf", [128, GH * NC], "float32"),
+    "rf": ("sbuf", [128, GH * NC], "float32"),
     "out": ("sbuf", [128, GH * NC], "float32"),
 }
-SEMAPHORES = ["ldx", "ldw", "qx", "qw", "sent", "mm0", "mm1", "ev0", "ev1", "st0", "st1"] + ["a%d" % r for r in range(N)]
+SEMAPHORES = (["ldx", "ldw", "qx", "qw", "sent", "hs", "hq", "c0", "c1", "e0", "e1", "st0", "st1"]
+              + ["x%d" % j for j in range(GR)] + ["m%d" % j for j in range(GR)] + ["f%d" % j for j in range(GH)])
 
 
 def _rank(i, k):
     return i * GC + k
 
 
-def _x_sources(r):
-    c = r % GC
-    return [_rank(g, k) for g in range(c * GH, (c + 1) * GH) for k in range(GC)]
+def _fellow(i):
+    return i // GH * GH + (i + 1) % GH
 
 
-def _w_sources(r):
-    return [_rank(r // GC, k) for k in range(GC)]
+def _first(i):
+    return (i + GH) % GR
 
 
-def _landing(r):
-    xs = [s for s in _x_sources(r) if s != r]
-    ws = [s for s in _w_sources(r) if s != r]
-    order = [("x", s) for s in xs if s not in ws]
-    for s in ws:
-        if s in xs:
-            order.append(("x", s))
-        order.append(("w", s))
-    return {key: U * j for j, key in enumerate(order)}
+def _slot(j, i):
+    return [_first(j), _fellow(_first(j)), _fellow(j)].index(i) * U
 
 
-def _calls(s):
-    xd = [d for d in range(N) if d != s and s in _x_sources(d)]
-    wd = [d for d in range(N) if d != s and s in _w_sources(d)]
-
-    def x_to(ds):
-        return (0, U, [(d, _landing(d)[("x", s)]) for d in ds])
-    if [d for d in wd if d in xd]:
-        calls = [x_to([d for d in xd if d not in wd and d not in _x_sources(d)])]
-        calls += [(0, 2 * U, [(d, _landing(d)[("x", s)])]) for d in wd]
-        calls += [x_to([d for d in xd if d not in wd and d in _x_sources(d)])]
-    else:
-        calls = [(U, 2 * U, [(d, _landing(d)[("w", s)])]) for d in wd] + [x_to(xd)]
-    out, sent = [], 0
-    for a, b, dests in calls:
-        sent += (b - a) // U * len(dests)
-        out.append((a, b, dests, sent))
-    return out
-
-
-def _mask(topo, cores, s, dests):
-    m = topo.mask(cores[s], cores[dests[0][0]])
-    for d, _ in dests:
-        m &= topo.mask(cores[s], cores[d])
-    return m
+def _helper(topo, c, d):
+    for h in range(WORLD):
+        if topo.host(h) == topo.host(c) and topo.chip(h) == topo.chip(c) and topo.die(h) != topo.die(c) and topo.may_write(h, d):
+            return h
+    return None
 
 
 def _ones(m):
     return bin(m).count("1")
 
 
+def _send(g, core, T, topo, src, dests, mask, rsem):
+    ids = []
+    for d, _ in dests:
+        rid, pid = topo.addr(d, core)
+        ids.append(DstId(rid=rid, pnc=pid))
+    g.remote_dma_fused([RemoteDMATransfer(dst_ids=ids, dma_engine_mask=mask, remote_sem=rsem, srcs=[src],
+                                          dsts=[ap for _, ap in dests])], local_sem=T.sem.sent)
+    return _ones(mask)
+
+
+def _masks(topo, T, r):
+    i, k = r // GC, r % GC
+    c = T.cores[r]
+    off = topo.mask(c, T.cores[_rank(_first(i), k)]) & topo.mask(c, T.cores[_rank(_fellow(_first(i)), k)])
+    h = _helper(topo, c, T.cores[_rank(_fellow(i), k)])
+    on = topo.mask(c, h) & ~off
+    if _ones(on) not in (1, 2, 4, 8, 16):
+        on = topo.mask(c, h)
+    return off, h, on
+
+
+def _relay(g, core, T, topo, r):
+    sem = T.sem
+    i, k = r // GC, r % GC
+    j = _fellow(i)
+    d = T.cores[_rank(j, k)]
+    n = _ones(_masks(topo, T, r)[2])
+    m = topo.mask(core, d)
+    o = _slot(j, i)
+    g.wait_ge(sem.hs, n)
+    left = _send(g, core, T, topo, T.rs[:, 0:U], [(d, T.rs[:, o:o + U])], m, sem["x%d" % i])
+    g.wait_ge(sem.hq, n)
+    left += _send(g, core, T, topo, T.rq[:, 0:U].bitcast(dt.uint8), [(d, T.rq[:, o:o + U].bitcast(dt.uint8))], m, sem["x%d" % i])
+    g.wait_ge(sem.sent, left)
+
+
 def rank_program(g, core, T, topo):
     r = T.rank_of(core)
     if r is None:
+        for s in range(N):
+            if _masks(topo, T, s)[1] == core:
+                _relay(g, core, T, topo, s)
         return
-    i, c = r // GC, r % GC
     sem = T.sem
-    calls = _calls(r)
+    i, k = r // GC, r % GC
+    a, b, f = _first(i), _fellow(_first(i)), _fellow(i)
+    keeps_own = i // GH == k
+    partner = T.cores[_rank(i, (k + 1) % GC)]
+    off, helper, on = _masks(topo, T, r)
 
-    inputs = [("x", T.x, T.xin, 0), ("w", T.w, T.win, U)]
-    if calls[0][0] >= U:
-        inputs.reverse()
-    for name, src, tile, off in inputs:
-        g.sync.dma_start(tile[:], src[:]).then_inc(sem["ld" + name], 16)
-    for name, src, tile, off in inputs:
+    g.sync.dma_start(T.xin[:], T.x[:]).then_inc(sem.ldx, 16)
+    g.sync.dma_start(T.win[:], T.w[:]).then_inc(sem.ldw, 16)
+    for name, tile, o0 in (("x", T.xin, 0), ("w", T.win, U)):
         g.vector.wait_ge(sem["ld" + name], 16)
         for t in range(KT):
-            o = off + NC * t
+            o = o0 + NC * t
             g.vector.quantize_mx(T.q[:, o:o + NC], T.s[:, o:o + NC], tile[:, 4 * NC * t:4 * NC * (t + 1)]).then_inc(sem["q" + name], 1)
 
-    left = 0
-    ready = set()
-    for a, b, dests, _ in calls:
-        for name, need in (("qx", a < U), ("qw", b > U)):
-            if need and name not in ready:
-                ready.add(name)
-                g.wait_ge(sem[name], KT)
-        m = _mask(topo, T.cores, r, dests)
-        ids = []
-        for d, _ in dests:
-            rid, pid = topo.addr(T.cores[d], core)
-            ids.append(DstId(rid=rid, pnc=pid))
-        g.remote_dma_fused([RemoteDMATransfer(
-            dst_ids=ids, dma_engine_mask=m, remote_sem=sem["a%d" % r],
-            srcs=[T.s[:, a:b]], dsts=[T.rs[:, o:o + b - a] for _, o in dests])], local_sem=sem.sent)
-        g.remote_dma_fused([RemoteDMATransfer(
-            dst_ids=ids, dma_engine_mask=m, remote_sem=sem["a%d" % r],
-            srcs=[T.q[:, a:b].bitcast(dt.uint8)], dsts=[T.rq[:, o:o + b - a].bitcast(dt.uint8) for _, o in dests])], local_sem=sem.sent)
-        left += 2 * _ones(m)
+    mine = sem["x%d" % i]
+    g.wait_ge(sem.qx, KT)
+    left = _send(g, core, T, topo, T.s[:, 0:U],
+                 [(T.cores[_rank(j, k)], T.rs[:, _slot(j, i):_slot(j, i) + U]) for j in (a, b)], off, mine)
+    left += _send(g, core, T, topo, T.q[:, 0:U].bitcast(dt.uint8),
+                  [(T.cores[_rank(j, k)], T.rq[:, _slot(j, i):_slot(j, i) + U].bitcast(dt.uint8)) for j in (a, b)], off, mine)
+    left += _send(g, core, T, topo, T.s[:, 0:U], [(helper, T.rs[:, 0:U])], on, sem.hs)
+    left += _send(g, core, T, topo, T.q[:, 0:U].bitcast(dt.uint8), [(helper, T.rq[:, 0:U].bitcast(dt.uint8))], on, sem.hq)
 
-    land = _landing(r)
-    arrive = {}
-    for s in range(N):
-        for a, b, dests, sent in _calls(s):
-            if s != r and r in [d for d, _ in dests]:
-                arrive[s] = (2 * _ones(_mask(topo, T.cores, s, dests)), sent)
-    prods = []
-    for gi in range(GH):
-        for k in range(GC):
-            xs, ws = _rank(c * GH + gi, k), _rank(i, k)
-            prods.append((max([arrive[s][1] for s in (xs, ws) if s != r] + [0]), gi, xs, ws))
-    prods.sort()
-    done = set()
-    count = [0] * GH
-    finish = []
-    for _, gi, xs, ws in prods:
-        for name, s in (("qx", xs), ("qw", ws)):
-            key = name if s == r else s
-            if key not in done:
-                done.add(key)
-                if s == r:
-                    g.tensor.wait_ge(sem[name], KT)
-                else:
-                    g.tensor.wait_ge(sem["a%d" % s], arrive[s][0])
+    n_in = {}
+    for j in (a, b):
+        n_in[j] = 2 * _ones(_masks(topo, T, _rank(j, k))[0])
+    n_in[f] = 2 * _ones(topo.mask(_masks(topo, T, _rank(f, k))[1], core))
+    g.tensor.wait_ge(sem.qx, KT)
+    g.tensor.wait_ge(sem.qw, KT)
+    for gg in ([i, a, b, f] if keeps_own else [i, a, f, b]):
+        if gg == i:
+            xq, xs, xo = T.q, T.s, 0
+        else:
+            xq, xs, xo = T.rq, T.rs, _slot(i, gg)
+            g.tensor.wait_ge(sem["x%d" % gg], n_in[gg])
         for t in range(KT):
-            if ws == r:
-                wq, wsc, wo = T.q, T.s, U + NC * t
-            else:
-                wq, wsc, wo = T.rq, T.rs, land[("w", ws)] + NC * t
-            if xs == r:
-                xq, xsc, xo = T.q, T.s, NC * t
-            else:
-                xq, xsc, xo = T.rq, T.rs, land[("x", xs)] + NC * t
-            count[gi] += 1
-            mm = g.tensor.matmul_mx(T.acc[:, 512 * gi:512 * gi + NC], wq[:, wo:wo + NC], wsc[:, wo:wo + NC],
-                                    xq[:, xo:xo + NC], xsc[:, xo:xo + NC], count[gi] == 1, count[gi] == GC * KT)
-            if count[gi] == GC * KT:
-                mm.then_inc(sem["mm%d" % len(finish)], 1)
-                finish.append(gi)
+            mm = g.tensor.matmul_mx(T.acc[:, 512 * gg:512 * gg + NC], T.q[:, U + NC * t:U + NC * (t + 1)], T.s[:, U + NC * t:U + NC * (t + 1)],
+                                    xq[:, xo + NC * t:xo + NC * (t + 1)], xs[:, xo + NC * t:xo + NC * (t + 1)], t == 0, t == KT - 1)
+        mm.then_inc(sem["m%d" % gg], 1)
 
-    gi = finish[0]
-    g.vector.wait_ge(sem.mm0, 1)
-    g.vector.tensor_copy(T.out[:, NC * gi:NC * gi + NC], T.acc[:, 512 * gi:512 * gi + NC]).then_inc(sem.ev0, 1)
-    g.sync.wait_ge(sem.ev0, 1)
-    g.sync.dma_start(T.y[:, NC * gi:NC * gi + NC], T.out[:, NC * gi:NC * gi + NC]).then_inc(sem.st0, 16)
-    gi = finish[1]
-    g.scalar.wait_ge(sem.mm1, 1)
-    g.scalar.activation(T.out[:, NC * gi:NC * gi + NC], T.acc[:, 512 * gi:512 * gi + NC], ActivationFunctionType.Copy).then_inc(sem.ev1, 1)
-    g.scalar.wait_ge(sem.ev1, 1)
-    g.scalar.dma_start(T.y[:, NC * gi:NC * gi + NC], T.out[:, NC * gi:NC * gi + NC]).then_inc(sem.st1, 16)
+    fmask = topo.mask(core, partner)
+    for n, gg in enumerate([a, b] if keeps_own else [i, f]):
+        o = NC * (gg % GH)
+        g.scalar.wait_ge(sem["m%d" % gg], 1)
+        g.scalar.activation(T.fo[:, o:o + NC], T.acc[:, 512 * gg:512 * gg + NC], ActivationFunctionType.Copy).then_inc(sem["c%d" % n], 1)
+        g.wait_ge(sem["c%d" % n], 1)
+        left += _send(g, core, T, topo, T.fo[:, o:o + NC], [(partner, T.rf[:, o:o + NC])], fmask, sem["f%d" % (gg % GH)])
+
+    n_f = _ones(topo.mask(partner, core))
+    for n, gg in enumerate([i, f] if keeps_own else [a, b]):
+        o = NC * (gg % GH)
+        g.vector.wait_ge(sem["m%d" % gg], 1)
+        g.vector.wait_ge(sem["f%d" % (gg % GH)], n_f)
+        g.vector.tensor_tensor(T.out[:, o:o + NC], T.acc[:, 512 * gg:512 * gg + NC], T.rf[:, o:o + NC], AluOpType.add).then_inc(sem["e%d" % n], 1)
+        qu = g.sync if n == 0 else g.scalar
+        qu.wait_ge(sem["e%d" % n], 1)
+        qu.dma_start(T.y[:, o:o + NC], T.out[:, o:o + NC]).then_inc(sem["st%d" % n], 16)
     g.sync.wait_ge(sem.st0, 16)
     g.scalar.wait_ge(sem.st1, 16)
     g.wait_ge(sem.sent, left)

@@ -1,26 +1,26 @@
 from concourse.bass import DstId, RemoteDMATransfer
-from concourse.mybir import dt, ActivationFunctionType, AluOpType
+from concourse.mybir import dt, ActivationFunctionType
 
 GR, GC, KT, NC = 4, 2, 2, 128
 N = GR * GC
 WORLD = 256
 U = KT * NC
 GH = GR // GC
+SLOTS = 5
+PIECES = {0: 3, 1: 2, 2: 2, 3: 3, 4: 3}
 
 SCRATCH = {
     "xin": ("sbuf", [128, 4 * U], "bfloat16"),
     "win": ("sbuf", [128, 4 * U], "bfloat16"),
     "q": ("sbuf", [128, 2 * U], "float8_e4m3fn_x4"),
     "s": ("sbuf", [128, 2 * U], "uint8"),
-    "rq": ("sbuf", [128, (GR - 1) * U], "float8_e4m3fn_x4"),
-    "rs": ("sbuf", [128, (GR - 1) * U], "uint8"),
-    "acc": ("psum", [128, 512 * GR], "float32"),
-    "fo": ("sbuf", [128, GH * NC], "float32"),
-    "rf": ("sbuf", [128, GH * NC], "float32"),
+    "rq": ("sbuf", [128, SLOTS * U], "float8_e4m3fn_x4"),
+    "rs": ("sbuf", [128, SLOTS * U], "uint8"),
+    "acc": ("psum", [128, 512 * GH], "float32"),
     "out": ("sbuf", [128, GH * NC], "float32"),
 }
-SEMAPHORES = (["ldx", "ldw", "qx", "qw", "sent", "hs", "hq", "c0", "c1", "e0", "e1", "st0", "st1"]
-              + ["x%d" % j for j in range(GR)] + ["m%d" % j for j in range(GR)] + ["f%d" % j for j in range(GH)])
+SEMAPHORES = (["ldx0", "ldx1", "ldw", "qx0", "qx1", "qw", "sent", "hs", "hq0", "hq1", "m0", "m1", "c0", "c1", "st0", "st1"]
+              + ["r%d" % j for j in range(SLOTS)])
 
 
 def _rank(i, k):
@@ -35,54 +35,90 @@ def _first(i):
     return (i + GH) % GR
 
 
-def _slot(j, i):
-    return [_first(j), _fellow(_first(j)), _fellow(j)].index(i) * U
+def _routes(i, k):
+    c = i // GH
+    a, b, f = _first(i), _fellow(_first(i)), _fellow(i)
+    if k == c:
+        return c, [(a, 0), (b, 2)], [(f, 3)]
+    return c, [(f, 0), (i, 2)], [(a, 3), (b, 4)]
 
 
-def _helper(topo, c, d):
-    for h in range(WORLD):
-        if topo.host(h) == topo.host(c) and topo.chip(h) == topo.chip(c) and topo.die(h) != topo.die(c) and topo.may_write(h, d):
-            return h
-    return None
+def _helpers(topo, T, r):
+    c, _, far = _routes(r // GC, r % GC)
+    me = T.cores[r]
+    res = []
+    for row, slot in far:
+        d = T.cores[_rank(row, c)]
+        for h in range(WORLD):
+            if (topo.host(h) == topo.host(me) and topo.chip(h) == topo.chip(me) and topo.die(h) != topo.die(me)
+                    and topo.may_write(h, d) and h not in [e[0] for e in res]):
+                res.append((h, d, slot))
+                break
+    return res
 
 
 def _ones(m):
     return bin(m).count("1")
 
 
-def _send(g, core, T, topo, src, dests, mask, rsem):
+def _masks(topo, T, r):
+    i, k = r // GC, r % GC
+    me = T.cores[r]
+    c, near, _ = _routes(i, k)
+    off = topo.mask(me, T.cores[_rank(i, (k + 1) % GC)])
+    for row, _ in near:
+        off &= topo.mask(me, T.cores[_rank(row, c)])
+    full = off | ~off
+    for h, _, _ in _helpers(topo, T, r):
+        full &= topo.mask(me, h)
+    on = full & ~off
+    if _ones(on) not in (1, 2, 4, 8, 16):
+        on = full
+    return off, on
+
+
+def _writers(topo, T, r):
+    res = {1: T.cores[_rank(r // GC, (r % GC + 1) % GC)]}
+    for s in range(N):
+        c, near, _ = _routes(s // GC, s % GC)
+        for row, slot in near:
+            if _rank(row, c) == r:
+                res[slot] = T.cores[s]
+        for h, d, slot in _helpers(topo, T, s):
+            if d == T.cores[r]:
+                res[slot] = h
+    return res
+
+
+def _send(g, core, T, topo, kind, src, lo, hi, dests, mask, rsem):
+    where, unit = src
+    if kind == "s":
+        sb = T.s if where == "own" else T.rs
+        sap = sb[:, U * unit + lo:U * unit + hi]
+        daps = [T.rs[:, U * sl + lo:U * sl + hi] for _, sl in dests]
+    else:
+        sb = T.q if where == "own" else T.rq
+        sap = sb[:, U * unit + lo:U * unit + hi].bitcast(dt.uint8)
+        daps = [T.rq[:, U * sl + lo:U * sl + hi].bitcast(dt.uint8) for _, sl in dests]
     ids = []
     for d, _ in dests:
         rid, pid = topo.addr(d, core)
         ids.append(DstId(rid=rid, pnc=pid))
-    g.remote_dma_fused([RemoteDMATransfer(dst_ids=ids, dma_engine_mask=mask, remote_sem=rsem, srcs=[src],
-                                          dsts=[ap for _, ap in dests])], local_sem=T.sem.sent)
+    g.remote_dma_fused([RemoteDMATransfer(dst_ids=ids, dma_engine_mask=mask, remote_sem=rsem, srcs=[sap], dsts=daps)],
+                       local_sem=T.sem.sent)
     return _ones(mask)
 
 
-def _masks(topo, T, r):
-    i, k = r // GC, r % GC
-    c = T.cores[r]
-    off = topo.mask(c, T.cores[_rank(_first(i), k)]) & topo.mask(c, T.cores[_rank(_fellow(_first(i)), k)])
-    h = _helper(topo, c, T.cores[_rank(_fellow(i), k)])
-    on = topo.mask(c, h) & ~off
-    if _ones(on) not in (1, 2, 4, 8, 16):
-        on = topo.mask(c, h)
-    return off, h, on
-
-
-def _relay(g, core, T, topo, r):
+def _relay(g, core, T, topo, n, d, slot):
     sem = T.sem
-    i, k = r // GC, r % GC
-    j = _fellow(i)
-    d = T.cores[_rank(j, k)]
-    n = _ones(_masks(topo, T, r)[2])
     m = topo.mask(core, d)
-    o = _slot(j, i)
+    rs = sem["r%d" % slot]
+    g.wait_ge(sem.hq0, n)
+    left = _send(g, core, T, topo, "q", ("got", 0), 0, NC, [(d, slot)], m, rs)
     g.wait_ge(sem.hs, n)
-    left = _send(g, core, T, topo, T.rs[:, 0:U], [(d, T.rs[:, o:o + U])], m, sem["x%d" % i])
-    g.wait_ge(sem.hq, n)
-    left += _send(g, core, T, topo, T.rq[:, 0:U].bitcast(dt.uint8), [(d, T.rq[:, o:o + U].bitcast(dt.uint8))], m, sem["x%d" % i])
+    left += _send(g, core, T, topo, "s", ("got", 0), 0, U, [(d, slot)], m, rs)
+    g.wait_ge(sem.hq1, n)
+    left += _send(g, core, T, topo, "q", ("got", 0), NC, U, [(d, slot)], m, rs)
     g.wait_ge(sem.sent, left)
 
 
@@ -90,67 +126,88 @@ def rank_program(g, core, T, topo):
     r = T.rank_of(core)
     if r is None:
         for s in range(N):
-            if _masks(topo, T, s)[1] == core:
-                _relay(g, core, T, topo, s)
+            for h, d, slot in _helpers(topo, T, s):
+                if h == core:
+                    _relay(g, core, T, topo, _ones(_masks(topo, T, s)[1]), d, slot)
         return
     sem = T.sem
     i, k = r // GC, r % GC
     a, b, f = _first(i), _fellow(_first(i)), _fellow(i)
-    keeps_own = i // GH == k
     partner = T.cores[_rank(i, (k + 1) % GC)]
-    off, helper, on = _masks(topo, T, r)
+    off, on = _masks(topo, T, r)
+    c, near, _ = _routes(i, k)
 
-    g.sync.dma_start(T.xin[:], T.x[:]).then_inc(sem.ldx, 16)
+    for t in range(KT):
+        g.sync.dma_start(T.xin[:, 4 * NC * t:4 * NC * (t + 1)], T.x[:, 4 * NC * t:4 * NC * (t + 1)]).then_inc(sem["ldx%d" % t], 16)
     g.sync.dma_start(T.win[:], T.w[:]).then_inc(sem.ldw, 16)
-    for name, tile, o0 in (("x", T.xin, 0), ("w", T.win, U)):
-        g.vector.wait_ge(sem["ld" + name], 16)
-        for t in range(KT):
-            o = o0 + NC * t
-            g.vector.quantize_mx(T.q[:, o:o + NC], T.s[:, o:o + NC], tile[:, 4 * NC * t:4 * NC * (t + 1)]).then_inc(sem["q" + name], 1)
+    for t in range(KT):
+        g.vector.wait_ge(sem["ldx%d" % t], 16)
+        g.vector.quantize_mx(T.q[:, NC * t:NC * (t + 1)], T.s[:, NC * t:NC * (t + 1)],
+                             T.xin[:, 4 * NC * t:4 * NC * (t + 1)]).then_inc(sem["qx%d" % t], 1)
+    g.vector.wait_ge(sem.ldw, 16)
+    for t in range(KT):
+        o = U + NC * t
+        g.vector.quantize_mx(T.q[:, o:o + NC], T.s[:, o:o + NC], T.win[:, 4 * NC * t:4 * NC * (t + 1)]).then_inc(sem.qw, 1)
 
-    mine = sem["x%d" % i]
-    g.wait_ge(sem.qx, KT)
-    left = _send(g, core, T, topo, T.s[:, 0:U],
-                 [(T.cores[_rank(j, k)], T.rs[:, _slot(j, i):_slot(j, i) + U]) for j in (a, b)], off, mine)
-    left += _send(g, core, T, topo, T.q[:, 0:U].bitcast(dt.uint8),
-                  [(T.cores[_rank(j, k)], T.rq[:, _slot(j, i):_slot(j, i) + U].bitcast(dt.uint8)) for j in (a, b)], off, mine)
-    left += _send(g, core, T, topo, T.s[:, 0:U], [(helper, T.rs[:, 0:U])], on, sem.hs)
-    left += _send(g, core, T, topo, T.q[:, 0:U].bitcast(dt.uint8), [(helper, T.rq[:, 0:U].bitcast(dt.uint8))], on, sem.hq)
+    hl = [(h, 0) for h, _, _ in _helpers(topo, T, r)]
+    d1 = [(T.cores[_rank(near[0][0], c)], near[0][1])]
+    d3 = [(T.cores[_rank(near[1][0], c)], near[1][1])]
+    s1, s3 = sem["r%d" % near[0][1]], sem["r%d" % near[1][1]]
+    X, W = ("own", 0), ("own", 1)
+    g.wait_ge(sem.qx0, 1)
+    left = _send(g, core, T, topo, "q", X, 0, NC, hl, on, sem.hq0)
+    left += _send(g, core, T, topo, "q", X, 0, NC, d1, off, s1)
+    g.wait_ge(sem.qx1, 1)
+    left += _send(g, core, T, topo, "s", X, 0, U, hl, on, sem.hs)
+    left += _send(g, core, T, topo, "q", X, NC, U, hl, on, sem.hq1)
+    left += _send(g, core, T, topo, "s", X, 0, U, d1, off, s1)
+    left += _send(g, core, T, topo, "q", X, NC, U, d1, off, s1)
+    g.wait_ge(sem.qw, KT)
+    left += _send(g, core, T, topo, "s", W, 0, U, [(partner, 1)], off, sem.r1)
+    left += _send(g, core, T, topo, "q", W, 0, U, [(partner, 1)], off, sem.r1)
+    left += _send(g, core, T, topo, "s", X, 0, U, d3, off, s3)
+    left += _send(g, core, T, topo, "q", X, 0, U, d3, off, s3)
 
-    n_in = {}
-    for j in (a, b):
-        n_in[j] = 2 * _ones(_masks(topo, T, _rank(j, k))[0])
-    n_in[f] = 2 * _ones(topo.mask(_masks(topo, T, _rank(f, k))[1], core))
-    g.tensor.wait_ge(sem.qx, KT)
+    if i // GH == k:
+        seq = [(i, None, None), (f, 1, 0), (f, None, 3), (i, 1, 2)]
+    else:
+        seq = [(a, None, 0), (a, 1, 3), (b, None, 2), (b, 1, 4)]
+    wr = _writers(topo, T, r)
     g.tensor.wait_ge(sem.qw, KT)
-    for gg in ([i, a, b, f] if keeps_own else [i, a, f, b]):
-        if gg == i:
-            xq, xs, xo = T.q, T.s, 0
-        else:
-            xq, xs, xo = T.rq, T.rs, _slot(i, gg)
-            g.tensor.wait_ge(sem["x%d" % gg], n_in[gg])
+    seen, begun, done = [], [], []
+    for gg, ws, xs in seq:
+        if xs is None:
+            g.tensor.wait_ge(sem.qx0, 1)
+            g.tensor.wait_ge(sem.qx1, 1)
+        for sl in (ws, xs):
+            if sl is not None and sl not in seen:
+                seen.append(sl)
+                g.tensor.wait_ge(sem["r%d" % sl], PIECES[sl] * _ones(topo.mask(wr[sl], core)))
+        wq, wp, wo = (T.q, T.s, U) if ws is None else (T.rq, T.rs, U * ws)
+        xq, xp, xo = (T.q, T.s, 0) if xs is None else (T.rq, T.rs, U * xs)
+        last = gg in begun
+        bank = 512 * (gg % GH)
         for t in range(KT):
-            mm = g.tensor.matmul_mx(T.acc[:, 512 * gg:512 * gg + NC], T.q[:, U + NC * t:U + NC * (t + 1)], T.s[:, U + NC * t:U + NC * (t + 1)],
-                                    xq[:, xo + NC * t:xo + NC * (t + 1)], xs[:, xo + NC * t:xo + NC * (t + 1)], t == 0, t == KT - 1)
-        mm.then_inc(sem["m%d" % gg], 1)
+            mm = g.tensor.matmul_mx(T.acc[:, bank:bank + NC], wq[:, wo + NC * t:wo + NC * (t + 1)], wp[:, wo + NC * t:wo + NC * (t + 1)],
+                                    xq[:, xo + NC * t:xo + NC * (t + 1)], xp[:, xo + NC * t:xo + NC * (t + 1)],
+                                    (not last) and t == 0, last and t == KT - 1)
+        if last:
+            mm.then_inc(sem["m%d" % len(done)], 1)
+            done.append(gg)
+        begun.append(gg)
 
-    fmask = topo.mask(core, partner)
-    for n, gg in enumerate([a, b] if keeps_own else [i, f]):
-        o = NC * (gg % GH)
-        g.scalar.wait_ge(sem["m%d" % gg], 1)
-        g.scalar.activation(T.fo[:, o:o + NC], T.acc[:, 512 * gg:512 * gg + NC], ActivationFunctionType.Copy).then_inc(sem["c%d" % n], 1)
-        g.wait_ge(sem["c%d" % n], 1)
-        left += _send(g, core, T, topo, T.fo[:, o:o + NC], [(partner, T.rf[:, o:o + NC])], fmask, sem["f%d" % (gg % GH)])
-
-    n_f = _ones(topo.mask(partner, core))
-    for n, gg in enumerate([i, f] if keeps_own else [a, b]):
-        o = NC * (gg % GH)
-        g.vector.wait_ge(sem["m%d" % gg], 1)
-        g.vector.wait_ge(sem["f%d" % (gg % GH)], n_f)
-        g.vector.tensor_tensor(T.out[:, o:o + NC], T.acc[:, 512 * gg:512 * gg + NC], T.rf[:, o:o + NC], AluOpType.add).then_inc(sem["e%d" % n], 1)
-        qu = g.sync if n == 0 else g.scalar
-        qu.wait_ge(sem["e%d" % n], 1)
-        qu.dma_start(T.y[:, o:o + NC], T.out[:, o:o + NC]).then_inc(sem["st%d" % n], 16)
-    g.sync.wait_ge(sem.st0, 16)
-    g.scalar.wait_ge(sem.st1, 16)
+    gg = done[0]
+    o, bank = NC * (gg % GH), 512 * (gg % GH)
+    g.scalar.wait_ge(sem.m0, 1)
+    g.scalar.activation(T.out[:, o:o + NC], T.acc[:, bank:bank + NC], ActivationFunctionType.Copy).then_inc(sem.c0, 1)
+    g.scalar.wait_ge(sem.c0, 1)
+    g.scalar.dma_start(T.y[:, o:o + NC], T.out[:, o:o + NC]).then_inc(sem.st0, 16)
+    gg = done[1]
+    o, bank = NC * (gg % GH), 512 * (gg % GH)
+    g.vector.wait_ge(sem.m1, 1)
+    g.vector.tensor_copy(T.out[:, o:o + NC], T.acc[:, bank:bank + NC]).then_inc(sem.c1, 1)
+    g.sync.wait_ge(sem.c1, 1)
+    g.sync.dma_start(T.y[:, o:o + NC], T.out[:, o:o + NC]).then_inc(sem.st1, 16)
+    g.scalar.wait_ge(sem.st0, 16)
+    g.sync.wait_ge(sem.st1, 16)
     g.wait_ge(sem.sent, left)

from concourse.bass import DstId, RemoteDMATransfer
from concourse.mybir import dt, ActivationFunctionType

GR, GC, KT, NC = 4, 2, 2, 128
N = GR * GC
WORLD = 256
U = KT * NC
GH = GR // GC
SLOTS = 5
PIECES = {0: 3, 1: 2, 2: 2, 3: 3, 4: 3}

SCRATCH = {
    "xin": ("sbuf", [128, 4 * U], "bfloat16"),
    "win": ("sbuf", [128, 4 * U], "bfloat16"),
    "q": ("sbuf", [128, 2 * U], "float8_e4m3fn_x4"),
    "s": ("sbuf", [128, 2 * U], "uint8"),
    "rq": ("sbuf", [128, SLOTS * U], "float8_e4m3fn_x4"),
    "rs": ("sbuf", [128, SLOTS * U], "uint8"),
    "acc": ("psum", [128, 512 * GH], "float32"),
    "out": ("sbuf", [128, GH * NC], "float32"),
}
SEMAPHORES = (["ldx0", "ldx1", "ldw", "qx0", "qx1", "qw", "sent", "hs", "hq0", "hq1", "m0", "m1", "c0", "c1", "st0", "st1"]
              + ["r%d" % j for j in range(SLOTS)])


def _rank(i, k):
    return i * GC + k


def _fellow(i):
    return i // GH * GH + (i + 1) % GH


def _first(i):
    return (i + GH) % GR


def _routes(i, k):
    c = i // GH
    a, b, f = _first(i), _fellow(_first(i)), _fellow(i)
    if k == c:
        return c, [(a, 0), (b, 2)], [(f, 3)]
    return c, [(f, 0), (i, 2)], [(a, 3), (b, 4)]


def _helpers(topo, T, r):
    c, _, far = _routes(r // GC, r % GC)
    me = T.cores[r]
    res = []
    for row, slot in far:
        d = T.cores[_rank(row, c)]
        for h in range(WORLD):
            if (topo.host(h) == topo.host(me) and topo.chip(h) == topo.chip(me) and topo.die(h) != topo.die(me)
                    and topo.may_write(h, d) and h not in [e[0] for e in res]):
                res.append((h, d, slot))
                break
    return res


def _ones(m):
    return bin(m).count("1")


def _masks(topo, T, r):
    i, k = r // GC, r % GC
    me = T.cores[r]
    c, near, _ = _routes(i, k)
    off = topo.mask(me, T.cores[_rank(i, (k + 1) % GC)])
    for row, _ in near:
        off &= topo.mask(me, T.cores[_rank(row, c)])
    full = off | ~off
    for h, _, _ in _helpers(topo, T, r):
        full &= topo.mask(me, h)
    on = full & ~off
    if _ones(on) not in (1, 2, 4, 8, 16):
        on = full
    return off, on


def _writers(topo, T, r):
    res = {1: T.cores[_rank(r // GC, (r % GC + 1) % GC)]}
    for s in range(N):
        c, near, _ = _routes(s // GC, s % GC)
        for row, slot in near:
            if _rank(row, c) == r:
                res[slot] = T.cores[s]
        for h, d, slot in _helpers(topo, T, s):
            if d == T.cores[r]:
                res[slot] = h
    return res


def _send(g, core, T, topo, kind, src, lo, hi, dests, mask, rsem):
    where, unit = src
    if kind == "s":
        sb = T.s if where == "own" else T.rs
        sap = sb[:, U * unit + lo:U * unit + hi]
        daps = [T.rs[:, U * sl + lo:U * sl + hi] for _, sl in dests]
    else:
        sb = T.q if where == "own" else T.rq
        sap = sb[:, U * unit + lo:U * unit + hi].bitcast(dt.uint8)
        daps = [T.rq[:, U * sl + lo:U * sl + hi].bitcast(dt.uint8) for _, sl in dests]
    ids = []
    for d, _ in dests:
        rid, pid = topo.addr(d, core)
        ids.append(DstId(rid=rid, pnc=pid))
    g.remote_dma_fused([RemoteDMATransfer(dst_ids=ids, dma_engine_mask=mask, remote_sem=rsem, srcs=[sap], dsts=daps)],
                       local_sem=T.sem.sent)
    return _ones(mask)


def _relay(g, core, T, topo, n, d, slot):
    sem = T.sem
    m = topo.mask(core, d)
    rs = sem["r%d" % slot]
    g.wait_ge(sem.hq0, n)
    left = _send(g, core, T, topo, "q", ("got", 0), 0, NC, [(d, slot)], m, rs)
    g.wait_ge(sem.hs, n)
    left += _send(g, core, T, topo, "s", ("got", 0), 0, U, [(d, slot)], m, rs)
    g.wait_ge(sem.hq1, n)
    left += _send(g, core, T, topo, "q", ("got", 0), NC, U, [(d, slot)], m, rs)
    g.wait_ge(sem.sent, left)


def rank_program(g, core, T, topo):
    r = T.rank_of(core)
    if r is None:
        for s in range(N):
            for h, d, slot in _helpers(topo, T, s):
                if h == core:
                    _relay(g, core, T, topo, _ones(_masks(topo, T, s)[1]), d, slot)
        return
    sem = T.sem
    i, k = r // GC, r % GC
    a, b, f = _first(i), _fellow(_first(i)), _fellow(i)
    partner = T.cores[_rank(i, (k + 1) % GC)]
    off, on = _masks(topo, T, r)
    c, near, _ = _routes(i, k)

    for t in range(KT):
        g.sync.dma_start(T.xin[:, 4 * NC * t:4 * NC * (t + 1)], T.x[:, 4 * NC * t:4 * NC * (t + 1)]).then_inc(sem["ldx%d" % t], 16)
    g.sync.dma_start(T.win[:], T.w[:]).then_inc(sem.ldw, 16)
    for t in range(KT):
        g.vector.wait_ge(sem["ldx%d" % t], 16)
        g.vector.quantize_mx(T.q[:, NC * t:NC * (t + 1)], T.s[:, NC * t:NC * (t + 1)],
                             T.xin[:, 4 * NC * t:4 * NC * (t + 1)]).then_inc(sem["qx%d" % t], 1)
    g.vector.wait_ge(sem.ldw, 16)
    for t in range(KT):
        o = U + NC * t
        g.vector.quantize_mx(T.q[:, o:o + NC], T.s[:, o:o + NC], T.win[:, 4 * NC * t:4 * NC * (t + 1)]).then_inc(sem.qw, 1)

    hl = [(h, 0) for h, _, _ in _helpers(topo, T, r)]
    d1 = [(T.cores[_rank(near[0][0], c)], near[0][1])]
    d3 = [(T.cores[_rank(near[1][0], c)], near[1][1])]
    s1, s3 = sem["r%d" % near[0][1]], sem["r%d" % near[1][1]]
    X, W = ("own", 0), ("own", 1)
    g.wait_ge(sem.qx0, 1)
    left = _send(g, core, T, topo, "q", X, 0, NC, hl, on, sem.hq0)
    left += _send(g, core, T, topo, "q", X, 0, NC, d1, off, s1)
    g.wait_ge(sem.qx1, 1)
    left += _send(g, core, T, topo, "s", X, 0, U, hl, on, sem.hs)
    left += _send(g, core, T, topo, "q", X, NC, U, hl, on, sem.hq1)
    left += _send(g, core, T, topo, "s", X, 0, U, d1, off, s1)
    left += _send(g, core, T, topo, "q", X, NC, U, d1, off, s1)
    g.wait_ge(sem.qw, KT)
    left += _send(g, core, T, topo, "s", W, 0, U, [(partner, 1)], off, sem.r1)
    left += _send(g, core, T, topo, "q", W, 0, U, [(partner, 1)], off, sem.r1)
    left += _send(g, core, T, topo, "s", X, 0, U, d3, off, s3)
    left += _send(g, core, T, topo, "q", X, 0, U, d3, off, s3)

    if i // GH == k:
        seq = [(i, None, None), (f, 1, 0), (f, None, 3), (i, 1, 2)]
    else:
        seq = [(a, None, 0), (a, 1, 3), (b, None, 2), (b, 1, 4)]
    wr = _writers(topo, T, r)
    g.tensor.wait_ge(sem.qw, KT)
    seen, begun, done = [], [], []
    for gg, ws, xs in seq:
        if xs is None:
            g.tensor.wait_ge(sem.qx0, 1)
            g.tensor.wait_ge(sem.qx1, 1)
        for sl in (ws, xs):
            if sl is not None and sl not in seen:
                seen.append(sl)
                g.tensor.wait_ge(sem["r%d" % sl], PIECES[sl] * _ones(topo.mask(wr[sl], core)))
        wq, wp, wo = (T.q, T.s, U) if ws is None else (T.rq, T.rs, U * ws)
        xq, xp, xo = (T.q, T.s, 0) if xs is None else (T.rq, T.rs, U * xs)
        last = gg in begun
        bank = 512 * (gg % GH)
        for t in range(KT):
            mm = g.tensor.matmul_mx(T.acc[:, bank:bank + NC], wq[:, wo + NC * t:wo + NC * (t + 1)], wp[:, wo + NC * t:wo + NC * (t + 1)],
                                    xq[:, xo + NC * t:xo + NC * (t + 1)], xp[:, xo + NC * t:xo + NC * (t + 1)],
                                    (not last) and t == 0, last and t == KT - 1)
        if last:
            mm.then_inc(sem["m%d" % len(done)], 1)
            done.append(gg)
        begun.append(gg)

    gg = done[0]
    o, bank = NC * (gg % GH), 512 * (gg % GH)
    g.scalar.wait_ge(sem.m0, 1)
    g.scalar.activation(T.out[:, o:o + NC], T.acc[:, bank:bank + NC], ActivationFunctionType.Copy).then_inc(sem.c0, 1)
    g.scalar.wait_ge(sem.c0, 1)
    g.scalar.dma_start(T.y[:, o:o + NC], T.out[:, o:o + NC]).then_inc(sem.st0, 16)
    gg = done[1]
    o, bank = NC * (gg % GH), 512 * (gg % GH)
    g.vector.wait_ge(sem.m1, 1)
    g.vector.tensor_copy(T.out[:, o:o + NC], T.acc[:, bank:bank + NC]).then_inc(sem.c1, 1)
    g.sync.wait_ge(sem.c1, 1)
    g.sync.dma_start(T.y[:, o:o + NC], T.out[:, o:o + NC]).then_inc(sem.st1, 16)
    g.scalar.wait_ge(sem.st0, 16)
    g.sync.wait_ge(sem.st1, 16)
    g.wait_ge(sem.sent, left)
